import numpy as np, ml_dtypes
CORES = [40,64,80,88,96,104,120,144]
N = 8
import mx_ref
BF = ml_dtypes.bfloat16
def gentries(a):
    return np.ascontiguousarray(a.reshape(8, 16, -1).transpose(0, 2, 1)).reshape(8, -1)
def gtable(e):
    e = np.asarray(e); return np.ascontiguousarray(e.reshape(8, -1, 16).transpose(0, 2, 1)).reshape(128, -1).astype(np.int32)
def gcols(t, e):
    v = np.concatenate([t.reshape(8, 16, -1, 4), np.zeros((8, 16, 1, 4), BF)], axis=2)
    return np.ascontiguousarray(np.stack([v[g][:, e[g]] for g in range(8)])).reshape(128, -1)
def tile(rs):
    return np.stack(rs, axis=2).reshape(128, -1).astype(BF)
def pick(q, e):
    c = np.concatenate([q[0].reshape(128, -1, 4), np.zeros((128, 1, 4), np.uint8)], axis=1); s = np.concatenate([q[1], np.ones((16, 1), np.uint8)], axis=1)
    return (np.ascontiguousarray(c[:, e].reshape(128, -1)), np.ascontiguousarray(s[:, e]))
def join(*qs):
    return (np.concatenate([q[0] for q in qs], axis=1), np.concatenate([q[1] for q in qs], axis=1))
def put(q, e, v):
    c, s = q[0].reshape(128, -1, 4).copy(), q[1].copy(); c[:, e] = v[0].reshape(128, -1, 4); s[:, e] = v[1]
    return (c.reshape(128, -1), s)
def pk(c, s):
    return (np.ascontiguousarray(c), mx_ref.live(s))
def emit(q):
    return q[0], q[1]
def packed(v, rng):
    q = [mx_ref.quantize(np.ascontiguousarray(v[r])) for r in range(N)]
    return np.stack([a for a, b in q]), np.stack([mx_ref.plane(b, rng) for a, b in q])
def values_of_codes():
    e, c = np.zeros((128, 128, 4), np.float32), np.zeros((128, 2, 4), np.uint8)
    e[np.arange(128), np.arange(128), 0] = 1
    c[:127, :, 0] = np.arange(256).reshape(2, 128).T[:127]
    return mx_ref.matmul(mx_ref.quantize(e.reshape(128, 512).astype(BF)), (c.reshape(128, 8), np.full((16, 2), 127, np.uint8))).T.reshape(-1).astype(np.float64)
CODE_VALUE, SCALE_VALUE = values_of_codes(), 2.0 ** (np.arange(256) - 127.0)
def decode(q):
    return (CODE_VALUE[q[0]].reshape(16, 8, -1, 4) * SCALE_VALUE[q[1]][:, None, :, None] + 0.0).reshape(128, -1).astype(np.float32)
def f(rng, *shape):
    return mx_ref.flush((rng.standard_normal(shape, dtype=np.float32) * np.exp2(rng.integers(-2, 3, shape[:-1] + (1,)))).astype(BF))
def wide(rng, *shape, cols=0):
    v = rng.standard_normal(shape, dtype=np.float32) * np.exp2(rng.integers(-12, 13, shape)).astype(np.float32)
    if cols: v *= np.repeat(np.exp2(rng.integers(-cols, cols + 1, shape[:-2] + (1, shape[-1] // 4))) * (rng.random(shape[:-2] + (1, shape[-1] // 4)) > 0.0625), 4, axis=-1).astype(np.float32)
    return mx_ref.flush(v.astype(BF))
C, E, R = 256, 128, 3
def parts(m):
    return np.repeat(np.repeat(m, 16, axis=0), 4, axis=1)
def big(v):
    v = v.astype(np.float32)
    v[np.abs(v) < np.float32(2.0 ** -16)] = 0
    return v.astype(BF)
def numbers_of(rng):
    return {"x": big(f(rng, N, 128, 4 * C)), "u": np.array(f(rng, N, 128, 512)), "v": np.array(f(rng, N, 128, 512))}
def layer(rng, still=0):
    w = big(f(rng, N, 128, 2048)).reshape(N, 8, 16, 4, 8, 16, 4)
    w[:, :, :, :, :, :still] = 0
    return w
def moved(rng, rows):
    w = np.zeros((N, 128, 4, 128, 4), np.float32)
    for r in range(N):
        h, e = 16 * rng.integers(8), rng.integers(4)
        for b in range(4): w[r, (rows + h) % 128, b, rows, (b + e) % 4] = rng.choice([-16.0, 16.0], len(rows))
    return w.astype(BF)
def weights(rng, w, m):
    wc, ws = packed(np.ascontiguousarray(w).reshape(N, 128, 2048), rng)
    mc, ms = packed(np.ascontiguousarray(m).reshape(N, 128, 2048), rng)
    return {"wc": wc, "ws": ws, "mc": mc, "ms": ms}
def orders(rng):
    return np.argsort(rng.random((N, 8, 2 * R, C)), axis=3)
def lists(e):
    return np.stack([gtable(e[r].reshape(8, -1)) for r in range(N)])
def signs(rng):
    return np.stack([rng.permutation(8) % 2 * 2.0 - 1.0 for r in range(N)])
def setup_inputs(rng):
    return {**numbers_of(rng), **weights(rng, layer(rng), layer(rng)), "pl": lists(orders(rng))}
def setup_inputs_ties(rng):
    d = numbers_of(rng)
    e = rng.permutation(N)
    x = d["x"].reshape(N, 8, 16, C, 4)
    for r in range(N):
        k = np.zeros(C, int) if r == e[0] else rng.permutation(C) % 3
        a = x[r][:, :8, :3].copy()
        a[:, :, 2] = 0
        x[r][:, :8] = a[:, :, k]
    x[e[1], :, :8] = 0
    u = d["u"].reshape(N, 8, 16, 128, 4)
    for k in range(3): u[:, :, 8:, k::16] = 0
    return {"x": x.reshape(N, 128, 4 * C), "u": u.reshape(N, 128, 512), "v": d["v"], **weights(rng, layer(rng, 8), layer(rng, 8)), "pl": lists(orders(rng))}
def setup_inputs_near(rng):
    d = numbers_of(rng)
    x = np.zeros((N, 8, 16, C, 4), np.float32)
    u = d["u"].reshape(N, 128, 128, 4)
    for k in range(3): u[:, :, k::16] = 0
    o = rng.permutation(N) % 4
    c = [signs(rng), signs(rng)]
    j = np.arange(C)
    for r in range(N):
        size, one = (1.0, 1.0) if o[r] < 2 else (2.0 ** -4, 2.0 ** -27)
        for k in range(2):
            a = np.where(rng.permutation(8) % 2 == 0, E - 1, rng.integers(0, E, 8))[:, None]
            s = ((j + a) % E + rng.integers(0, 2, (8, 1))) // 2
            s[:, E:] = E // 2 + 1
            g = ((s[:, :, None] >> np.arange(8)) & 1) * np.exp2(np.arange(8) - 23.0) * size
            top = E - 1 - rng.integers(0, E // 8, (8, 1))
            if o[r] == 3:
                high = (j == top) | (j == 0) | (j >= E)
                x[r, :, k, :, 0] = (8 + high) * 2.0 ** -30
                x[r, :, 4 + k, :, 0] = (9 - high) * 2.0 ** -30
            else:
                if o[r] < 2: x[r, :, k, :, 0] = c[k][r][:, None]
                x[r, :, 8 + 2 * k] = g[:, :, :4]
                x[r, :, 9 + 2 * k] = g[:, :, 4:]
        x[r, :, 2, :, 0] = rng.integers(-1, 2, (8, C)) * one
        if o[r] == 2:
            x[r, :, 3] = x[r, :, 2]
            x[r, :, 2] *= 1.125
        if o[r] == 3:
            for g in rng.permutation(8)[:4]: x[r, g, 2, :, 0] = one
        x[r, :, 12:] = rng.integers(4, 8, (8, 4, C, 4)) * rng.choice([-1.0, 1.0], (8, 4, C, 4)) * 2.0 ** -20
        z = 1.0 if o[r] == 0 else 2.0 ** -30
        for h in range(0, 128, 16):
            for k in range(3): u[r, h + k, h + k, 0] = z
            for k in range(2): u[r, h + 8 + 2 * k:h + 10 + 2 * k, h + k] = z
            if o[r] == 2: u[r, h + 3, h + 2, 0] = -z
            if o[r] == 3:
                for k in range(2):
                    u[r, h + k, h + k, 0] = 1.125 * z
                    u[r, h + 4 + k, h + k, 0] = z
    rows = np.flatnonzero(np.arange(128) % 16 >= 12)
    return {"x": x.reshape(N, 128, 4 * C).astype(BF), "u": u.reshape(N, 128, 512), "v": d["v"], **weights(rng, moved(rng, rows), moved(rng, rows)), "pl": lists(orders(rng))}
def setup_inputs_huge(rng):
    d = numbers_of(rng)
    c = np.ones((N, C))
    for r in rng.permutation(N)[:N // 2]: c[r] = rng.permutation(C) % 2 * 2.0 - 1.0
    x = 2.0 ** 30 * (0.8 + 0.2 * rng.random((N, 128, C, 4))) * c[:, None, :, None]
    u = d["u"].reshape(N, 128, 8, 16, 4)
    a = 2.0 ** 30 * (1 - 0.1 * rng.random((N, 128, 8, 3, 4))) * np.stack([signs(rng), signs(rng), signs(rng)], axis=2)[:, None, :, :, None]
    u[:, :, :, :3] = a.astype(np.float32).astype(BF)
    rows = np.arange(128)
    return {"x": x.astype(np.float32).reshape(N, 128, 4 * C).astype(BF), "u": u.reshape(N, 128, 512), "v": d["v"], **weights(rng, moved(rng, rows), moved(rng, rows)), "pl": lists(orders(rng))}
def setup_inputs_places(rng):
    d = numbers_of(rng)
    x = d["x"].reshape(N, 8, 16, C, 4)
    x[:, :, :8] = 0
    u = d["u"].reshape(N, 128, 128, 4)
    for k in range(3): u[:, :, k::16] = 0
    for h in range(0, 128, 16):
        for k in range(3): u[:, h + k, h + k, 0] = 1
    e = orders(rng)
    for r in range(N):
        b = [rng.permutation(np.array([1, 2, E // 2 - 1, E // 2, E // 2 + 1, E - 1, rng.integers(1, E), rng.integers(1, E)])) for k in range(2)]
        same, kinds = rng.permutation(8)[:4], rng.permutation(8)
        b[1][same] = b[0][same]
        for g in range(8):
            for k in range(2):
                s = rng.integers(8, 16, C) * 0.0625
                s[0], s[E:], s[b[k][g]] = 4, 4, 2
                x[r, g, k, :, 0] = s
            s = rng.integers(-1, 2, C)
            if kinds[g] < 3: s[:] = kinds[g] - 1
            if kinds[g] == 3: s = (np.arange(C) == rng.integers(C)) * 2 - 1
            x[r, g, 2, :, 0] = s
        for i in range(2 * R):
            h = (r + i) % 4
            if h == 0: e[r, :, i] = np.arange(C)
            if h == 1: e[r, :, i] = np.arange(C)[::-1]
            if h == 2: e[r, :, i] = e[r, 0, i].copy()
    return {"x": x.reshape(N, 128, 4 * C), "u": u.reshape(N, 128, 512), "v": d["v"], **weights(rng, layer(rng, 8), layer(rng, 8)), "pl": lists(e)}
def setup_inputs_spread(rng):
    d = setup_inputs(rng)
    d["x"] = big(wide(rng, N, 128, 4 * C, cols=6))
    return d
def check_inputs(d):
    b = []
    for k in ("x", "u", "v"):
        a = np.abs(d[k].astype(np.float32))
        if not (np.isfinite(a).all() and ((a == 0) | (a >= 2.0 ** -30) & (a <= 2.0 ** 30)).all()): b.append("a value of " + k)
    none, least, most = [emit(mx_ref.quantize(np.full((128, 16), k, np.float32).astype(BF)))[1][0, 0] for k in (0.0, 2.0 ** -30, 2.0 ** 30)]
    for c, s in (("wc", "ws"), ("mc", "ms")):
        if ((d[c] & 0x7F) == 0x7F).any(): b.append("a code of " + c + " that is no number")
        for r in range(N):
            a = mx_ref.live(d[s][r])
            if ((a != none) & ((a < least) | (a > most))).any(): b.append("a scale of " + s)
    for r in range(N):
        e = gentries(d["pl"][r]).reshape(8, 2 * R, C)
        if not (np.sort(e, axis=2) == np.arange(C)).all(): b.append("a list of pl that is no permutation")
    return b
def reference(x, u, v, wc, ws, mc, ms, pl):
    qu = [mx_ref.quantize(u[r]) for r in range(N)]
    lay = [[pk(wc[r], ws[r]), pk(mc[r], ms[r])] for r in range(N)]
    at = [gentries(pl[r]).reshape(8, 2 * R, C) for r in range(N)]
    now = [x[r] for r in range(N)]
    place = np.arange(C)
    od = np.zeros((N, 8, 2 * R), np.float32)
    for t in range(R):
        for r in range(N):
            far = (r + 1 + t) % N
            q = mx_ref.quantize(now[r])
            s = mx_ref.matmul(qu[r], q) + np.float32(0.0)
            turn = np.where(parts(s[2::16] > 0), np.float32(1.0), np.float32(-1.0))
            fold = (decode(q) * turn).astype(BF)
            own = now[r].astype(np.float32) * turn
            back = []
            for k in range(2):
                b = 1 + np.argmax(s[k::16, 1:E], axis=1)
                od[r, :, 2 * t + k] = b
                low = np.stack([place[place < place ^ j] for j in b])
                i = np.take_along_axis(at[r][:, 2 * t + k], low, axis=1)
                m = np.take_along_axis(at[r][:, 2 * t + k], low ^ b[:, None], axis=1)
                z = mx_ref.quantize(((gcols(fold, i).astype(np.float32) + gcols(fold, m).astype(np.float32)) * np.float32(0.5)).astype(BF))
                h = mx_ref.quantize(tile([mx_ref.matmul(pick(lay[far][k], np.arange(128 * j, 128 * j + 128)), z) * np.float32(0.03125) for j in range(4)]))
                n = np.zeros((8, C), int)
                for e in (i, m): np.put_along_axis(n, e, np.broadcast_to(np.arange(C // 2), (8, C // 2)), axis=1)
                back.append(gcols(decode(h).astype(BF), n).astype(np.float32))
            middle = np.maximum(np.minimum(back[0], back[1]), np.minimum(np.maximum(back[0], back[1]), own))
            now[r] = ((own + middle) * np.float32(0.5)).astype(BF)
    y = np.zeros((N, 128, C), np.float32)
    oc, osc = np.zeros((N, 128, 4 * C), np.uint8), np.zeros((N, 16, C), np.uint8)
    for r in range(N):
        q = mx_ref.quantize(now[r])
        y[r] = mx_ref.matmul(mx_ref.quantize(v[r]), q)
        oc[r], osc[r] = emit(q)
    return {"y": y, "od": od, "oc": oc, "osc": osc}

from concourse.bass import DstId, RemoteDMATransfer
from concourse.mybir import dt, AluOpType, ActivationFunctionType

ALU = AluOpType
ACT = ActivationFunctionType
R = 3
TS = 1
FP8, U8, BF, F32, I32, U16 = "float8_e4m3fn_x4", "uint8", "bfloat16", "float32", "int32", "uint16"
WIDTHS = {
    FP8: dict(wq=512, mq=512, wl=512, uq=128, ur=384, vq=128, e1q=512, ehq=512, xq=1024, zq=768, zl=768, hq=768, hl=768),
    U8: dict(wp=512, mp=512, wlp=512, up=128, urp=384, vp=128, e1p=512, ehp=512, xp=1024, zp=768, zlp=768, hp=768, hlp=768),
    BF: dict(x0=1024, ub=512, vb=512, one=128, half=128, e1=520, eh=520, c4=256, c16=256, jr=256, cr=256, plb=96, rp=1024, ew=3072,
             gr=512, sc=512, s16=512, pos=256, nr=256, nc=256, sp=256, sn=256, fl=256, sf=256, xt=1024, xx=2048, vt=1024, zlow=1024,
             zt=1024, ht=1024, yh=1024, yp=1024, d1=512, u0=2048, u1=2048, mm=2048),
    F32: dict(f=48, rw=184, dl=56, lo=64, hi=64, rd=32, tab=2048, j4=64, j16=64, ct=384, k16=64, ky=64, ty=64, cm=256, sg=128, cnt=6,
              odb=6, tn=256, yo=256),
    I32: dict(pli=96, pi=1, fi=8, ci=56),
    U16: dict(cu=56, to=4, pu=32, l64=128, l16=32, pl0=64, n1=64, ly=64),
}
SCRATCH = {name: ("sbuf", [128, w], d) for d in WIDTHS for name, w in WIDTHS[d].items()}
SCRATCH["ps"] = ("psum", [128, 4096], F32)
SEMAPHORES = (["ve", "ac", "pe", "po", "sent", "wa"] + ["%s%d%d" % (a, t, k) for a in "zh" for t in range(R) for k in range(2)]
              + ["d%d" % i for i in range(28)])


def count(m):
    return bin(m).count("1")


def messages(rank, T, topo):
    n, core = len(T.cores), T.cores[rank]
    hs = [c for c in topo.cores_of(core) if c != core and all(topo.may_write(c, d) for d in T.cores if d != core)]
    hs = [c for c in hs if topo.die(c) == topo.die(core)] + [c for c in hs if topo.die(c) != topo.die(core)]
    out = [("wa", T.cores[(rank - 1 - TS) % n],
            [(hs[0], ("wp", 0, 256), ("wlp", 0, 256)), (hs[1], ("wp", 256, 512), ("wlp", 256, 512)),
             (hs[2], ("wq", 0, 256), ("wl", 0, 256)), (hs[3], ("wq", 256, 512), ("wl", 256, 512))])]
    for t in range(R):
        for a, dst in (("z", T.cores[(rank + 1 + t) % n]), ("h", T.cores[(rank - 1 - t) % n])):
            for k in range(2):
                if t == TS and k == 0:
                    continue
                c = 128 * (2 * t + k)
                direct = topo.may_write(core, dst)
                out.append(("%s%d%d" % (a, t, k), dst, [(None if direct else hs[0], (a + "q", c, c + 128), (a + "l", c, c + 128)),
                                                        (None if direct else hs[1], (a + "p", c, c + 128), (a + "lp", c, c + 128))]))
    return out


def view(T, v):
    a = T[v[0]][:, v[1]:v[2]]
    return a.bitcast(dt.uint8) if SCRATCH[v[0]][2] == FP8 else a


def write(g, T, topo, src, dst, out, in_, sem):
    rid, pid = topo.addr(dst, src)
    m = topo.mask(src, dst)
    g.remote_dma(view(T, out), view(T, in_), T.sem[sem], T.sem.sent, pid, rid, m)
    return count(m)


def relay_program(g, core, T, topo):
    sent = 0
    for rank, c in enumerate(T.cores):
        if core in topo.cores_of(c):
            for sem, dst, parts in messages(rank, T, topo):
                for via, src, land in parts:
                    if via == core:
                        g.wait_ge(T.sem[sem], count(topo.mask(c, core)) // (len(parts) if sem == "wa" else 1))
                        sent += write(g, T, topo, core, dst, land, land, sem)
    if sent:
        g.wait_ge(T.sem.sent, sent)


def schedule(T, topo):
    n = len(T.cores)
    cost = {"pairs": 1.5, "positions": 1.5, "windows": 0.6, "bounds": 2.2}

    def way(a, b):
        return 3.0 if topo.may_write(T.cores[a], T.cores[b]) else 4.2
    start, plan = [0.0] * n, [[] for r in range(n)]
    for t in range(R):
        home = t == TS
        free, done = [0.0] * n, [None] * n
        for r in range(n):
            o = (r - 1 - t) % n
            comes = start[o] + 4.9 + way(o, r)
            now = start[r] + 6.3 + (1.0 if home else 0.0) + (0.0 if t else 1.9)
            rest = ["pairs", "positions"] + (["bounds"] if home else []) + (["windows"] if t + 1 < R else [])
            steps = []
            while rest and now + cost[rest[0]] < comes:
                now += cost[rest[0]]
                steps.append(rest.pop(0))
            one = max(now, comes) + 1.0
            two = one if home else max(one, comes + 1.2) + 1.0
            done[r] = (one, two)
            free[r] = two + sum(cost[s] for s in rest)
            plan[r].append(steps + ["lend"] + rest + ([] if home else ["bounds"]))
        for r in range(n):
            l = (r + 1 + t) % n
            bound = free[r] if home else max(free[r], done[l][0] + way(l, r)) + 2.4
            start[r] = max(bound, done[l][1] + way(l, r) + 1.4) + 2.8
    return plan


def rank_program(g, core, T, topo):
    rank = T.rank_of(core)
    if rank is None:
        relay_program(g, core, T, topo)
        return
    n = len(T.cores)
    V, A, P = g.vector, g.scalar, g.tensor
    queue = {"ve": V, "ac": A, "pe": P, "po": g, "sy": g.sync}
    known = {q: {} for q in queue}
    total, waited, wrote, read, banks = {}, {}, {}, {}, {}
    ndma = [0]

    def need(q, evs):
        best = {}
        for e in evs:
            if e is not None and known[q].get(e[0], 0) < e[1] and best.get(e[0], (0, 0))[1] < e[1]:
                best[e[0]] = e
        for e in sorted(best.values(), key=lambda e: -len(e[2])):
            if known[q].get(e[0], 0) >= e[1]:
                continue
            queue[q].wait_ge(T.sem[e[0]], e[1])
            waited[e[0]] = max(waited.get(e[0], 0), e[1])
            for s, c in list(e[2].items()) + [(e[0], e[1])]:
                if known[q].get(s, 0) < c:
                    known[q][s] = c

    def op(q, fn, r=(), w=(), bank=None, dma=False):
        evs = [wrote.get(x) for x in list(r) + list(w)]
        for x in w:
            evs += read.get(x, [])
        if bank is not None:
            evs += [e for o, e in banks.get(bank, {}).items() if o != q]
        need(q, evs)
        ins = fn()
        if dma:
            sem, inc = "d%d" % ndma[0], 16
            ndma[0] += 1
        else:
            sem, inc = q, 1
        ins.then_inc(T.sem[sem], inc)
        total[sem] = total.get(sem, 0) + inc
        e = (sem, total[sem], dict(known[q]))
        for x in r:
            read.setdefault(x, []).append(e)
        for x in w:
            wrote[x], read[x] = e, []
        if bank is not None:
            banks.setdefault(bank, {})[q] = e

    for o in range(n):
        for sem, dst, parts in messages(o, T, topo):
            if dst == core:
                total[sem] = sum(count(topo.mask(T.cores[o] if via is None else via, core)) for via, s, l in parts)
                wrote["in:" + sem] = (sem, total[sem], {})
    mine = {sem: (dst, parts) for sem, dst, parts in messages(rank, T, topo)}
    total["sent"] = 0

    def send(sem, key):
        dst, parts = mine[sem]
        need("po", [wrote[key]])
        for via, src, land in parts:
            total["sent"] += write(g, T, topo, core, dst if via is None else via, land, src, sem)

    def send_layer(i, key):
        parts, trs = mine["wa"][1], []
        need("po", [wrote[key]])
        for j in (i, i + 1):
            via, src, land = parts[j]
            es = topo.engines(core, via)
            q = len(es) // len(parts)
            rid, pid = topo.addr(via, core)
            trs.append(RemoteDMATransfer(dst_ids=[DstId(rid=rid, pnc=pid)], dma_engine_mask=sum(1 << e for e in es[q * j:q * j + q]),
                                         remote_sem=T.sem.wa, src=view(T, src), dst=view(T, land)))
            total["sent"] += q
        g.remote_dma_fused(trs, local_sem=T.sem.sent)

    def ts(out, in0, s1, s2, o0, o1=None, r=(), w=(), bank=None):
        if o1 is None:
            op("ve", lambda: V.tensor_scalar(out, in0, s1, None, o0), r, w, bank)
        else:
            op("ve", lambda: V.tensor_scalar(out, in0, s1, s2, o0, o1), r, w, bank)

    def tt(out, in0, in1, o, r=(), w=(), bank=None):
        op("ve", lambda: V.tensor_tensor(out, in0, in1, o), r, w, bank)

    def cp(out, in_, r=(), w=(), bank=None):
        op("ve", lambda: V.tensor_copy(out, in_), r, w, bank)

    def acp(out, in_, r=(), w=(), bank=None, scale=None):
        if scale is None:
            op("ac", lambda: A.activation(out, in_, ACT.Copy), r, w, bank)
        else:
            op("ac", lambda: A.activation(out, in_, ACT.Copy, scale=scale), r, w, bank)

    def lin(out, in_, scale, bias, r=(), w=()):
        op("ac", lambda: A.activation(out, in_, ACT.Identity, bias=bias, scale=scale), r, w)

    def iota(name, a, b, pattern, base, key, mult=0):
        if SCRATCH[name][2] == I32:
            op("po", lambda: g.iota(T[name][:, a:b], pattern, base, mult), (), [key])
        else:
            op("po", lambda: g.iota(T[name][:, a:b], pattern, base, mult, allow_small_or_imprecise_dtypes=True), (), [key])

    def fill(name, c):
        op("ve", lambda: V.memset(T[name][:], c), w=[name])

    def diagonal(e, c):
        op("po", lambda: g.affine_select(T[e][:, 3:515:4], T[c][:], [[-1, 128]], ALU.is_equal, 0.0, 0, 1), [c], [e])

    def quant(q, p, c0, c1, tile, r, w):
        op("ve", lambda: V.quantize_mx(T[q][:, c0:c1], T[p][:, c0:c1], tile), r, w)

    def mm(bank, lq, lp, l0, rq, rp, r0, cols, r):
        op("pe", lambda: P.matmul_mx(T.ps[:, 512 * bank:512 * bank + cols], T[lq][:, l0:l0 + 128], T[lp][:, l0:l0 + 128],
                                     T[rq][:, r0:r0 + cols], T[rp][:, r0:r0 + cols], True, True), r, (), bank)

    def scan(out, d0, d1, init, o0, o1, r, w, bank=None):
        op("ve", lambda: V.tensor_tensor_scan(out, d0, d1, init, o0, o1), r, w, bank)

    def dma(q, out, in_, r=(), w=()):
        op(q, lambda: queue[q].dma_start(out, in_), r, w, dma=True)

    def ps(bank, a, b):
        return T.ps[:, 512 * bank + a:512 * bank + b]

    def col(j):
        return T.f[:, j:j + 1]

    def fk(*js):
        return ["f%d" % j for j in js]

    def flin(o, i, scale, bias):
        lin(col(o), col(i), scale, col(bias[0]) if isinstance(bias, list) else bias, fk(i, *(bias if isinstance(bias, list) else [])), fk(o))

    plan = schedule(T, topo)
    first = [1 if t == TS else 0 for t in range(R)]

    dma("sy", T.wp[:], T.ws[:], w=["wp"])
    dma("sy", T.x0[:, 0:512], T.x[:, 0:512], w=["xa"])
    dma("ac", T.pli[:], T.pl[:], w=["pli"])
    dma("ac", T.ub[:], T.u[:], w=["ub"])
    dma("sy", T.x0[:, 512:1024], T.x[:, 512:1024], w=["xb"])
    dma("sy", T.wq[:].bitcast(dt.uint8), T.wc[:], w=["wq"])
    dma("sy", T.mq[:].bitcast(dt.uint8), T.mc[:], w=["mq"])
    dma("sy", T.mp[:], T.ms[:], w=["mp"])
    dma("sy", T.vb[:], T.v[:], w=["vb"])

    iota("pi", 0, 1, [[0, 1]], 0, "pi", 1)
    fill("one", 1.0)
    fill("e1", 0.0)
    iota("ci", 0, 24, [[1, 3], [16, 8]], 0, "cia")
    diagonal("e1", "one")
    iota("ci", 24, 56, [[1, 16], [0, 2]], 0, "cib")
    iota("j4", 0, 64, [[0, 16], [4, 4]], 0, "j4")
    iota("rw", 0, 128, [[0, 16], [1, 8]], 0, "il")
    iota("dl", 0, 8, [[0, 4], [-2, 2]], 1, "dl0")
    iota("dl", 8, 24, [[0, 4], [-4, 2], [0, 2]], 2, "dl1")
    iota("dl", 24, 56, [[0, 4], [-8, 2], [0, 4]], 4, "dl2")
    iota("lo", 0, 16, [[0, 2], [2, 8]], 0, "lo0")
    iota("lo", 16, 32, [[0, 2], [4, 4], [1, 2]], 0, "lo1")
    iota("lo", 32, 64, [[0, 4], [8, 2], [1, 4]], 0, "lo2")
    send_layer(0, "wp")
    send_layer(2, "wq")

    for j, m in enumerate((1, 2, 4, 8, 16, 15, 3, 12)):
        ts(T.fi[:, j:j + 1], T.pi[:], m, None, ALU.bitwise_and, r=["pi"], w=["fi%d" % j])
    cp(T.f[:, 0:8], T.fi[:], r=["fi%d" % j for j in range(8)], w=fk(*range(8)))
    cp(T.cu[:], T.ci[:], r=["cia", "cib"], w=["cu"])
    for b in range(4):
        quant("e1q", "e1p", 128 * b, 128 * b + 128, T.e1[:, 3 - b:515 - b], ["e1"], ["e1q%d" % b])
    W = (8, 32, 64, 128, 256)
    flin(8, 5, 32.0, [4])
    for j in range(3):
        flin(12 + (1 << j), j, -2.0 * W[j] / (1 << j), float(W[j]))
        flin(9 + j, j, -float(W[j + 1] - W[j]) / (1 << j), [8 + j])
    flin(15, 13, 1.0, [14])
    flin(12, 0, 0.0, 0.0)
    flin(29, 5, 1.0, 8.0)
    for j in range(1, 4):
        flin(19 + j, 8 + j, 1.0, float(W[j]))
    lin(T.f[:, 17:20], T.f[:, 13:16], 1.0, col(16), fk(13, 14, 15, 16), fk(17, 18, 19))
    flin(23, 3, 127.0, [29])
    flin(25, 6, 1.0, -4.0)
    lin(T.f[:, 32:40], T.f[:, 12:20], 1.0, col(22), fk(*range(12, 20)) + fk(22), ["hb"])
    ts(col(30), col(7), 0.0, 4096.0 - 2.0 ** -8, ALU.is_equal, ALU.mult, fk(7), fk(30))
    flin(24, 30, 1.0, 2.0 ** -8)

    def picker(name, j, c, step, top, o):
        ts(T.ct[:, o:o + 64], T[j][:], col(c), 1023.0, ALU.is_equal, ALU.mult, [j] + fk(c), [name + "a"])
        ts(T.ct[:, o + 64:o + 128], T[j][:], step, col(c), ALU.add, ALU.not_equal, [j] + fk(c), [name + "b"])
        ts(T.ct[:, o + 128:o + 192], T[j][:], top, col(c), ALU.subtract, ALU.is_equal, [j] + fk(c), [name + "c"])
        tt(T.ct[:, o:o + 64], T.ct[:, o:o + 64], T.ct[:, o + 64:o + 128], ALU.add, [name + "b"], [name + "a"])
        ts(T.ct[:, o + 128:o + 192], T.ct[:, o + 128:o + 192], 2.0 ** -20 - 1.0, None, ALU.mult, r=[], w=[name + "c"])
        tt(T[name][:, 0:64], T.ct[:, o:o + 64], T.ct[:, o + 128:o + 192], ALU.add, [name + "a", name + "c"], [name + "0"])
        cp(T[name][:, 64:128], T[name][:, 0:64], [name + "0"], [name + "1"])
        cp(T[name][:, 128:256], T[name][:, 0:128], [name + "0", name + "1"], [name])

    def window_a(t, k):
        c = 16 * (2 * t + k)
        acp(T.rp[:, 512 * k:512 * k + 512], T.plb[:, c:c + 16].indirect(T.cu[:, 24:56]), ["plb", "cu"], ["rp%d" % k])

    def window_b(t, k):
        c = 2 * t + k
        op("ve", lambda: V.transpose(T.ew[:, 512 * c:512 * c + 512], T.rp[:, 512 * k:512 * k + 512]), ["rp%d" % k], ["ew%d" % c])

    def upick(k):
        cp(T.ur[:, 128 * k:128 * k + 128].bitcast(dt.uint32), T.uq[:, 0:128].bitcast(dt.uint32).indirect(T.cu[:, 8 * k:8 * k + 8]),
           ["uq", "cu"], ["ur%d" % k])
        acp(T.urp[:, 128 * k:128 * k + 128], T.up[:, 0:128].indirect(T.cu[:, 8 * k:8 * k + 8]), ["uq", "cu"], ["us%d" % k])

    tabk, rk = [], ["il", "r1", "r2", "r3"]
    picker("c4", "j4", 7, 4.0, 12.0, 0)
    for a, b, h in [(64, 128, 0), (128, 256, 1), (256, 384, 2), (384, 512, 2)] + [(a, a + 128, 3) for a in range(512, 1024, 128)]:
        tabk.append("tl%d" % a)
        lin(T.tab[:, a:b], T.rw[:, 0:b - a], 1.0, col(8 + h), ["il"] + fk(8 + h), [tabk[-1]])
    tt(T.rw[:, 128:136], T.rw[:, 120:128], T.dl[:, 0:8], ALU.add, ["il", "dl0"], ["r1"])
    ts(T.plb[:], T.pli[:], 1.0, None, ALU.add, r=["pli"], w=["plb"])
    tt(T.rw[:, 136:152], T.rw[:, 120:136], T.dl[:, 8:24], ALU.add, ["il", "r1", "dl1"], ["r2"])
    tt(T.rw[:, 152:184], T.rw[:, 120:152], T.dl[:, 24:56], ALU.add, ["il", "r1", "r2", "dl2"], ["r3"])

    def table_high(which):
        for bh in which:
            h = bh.bit_length() - 1
            rest = bh - (1 << h)
            tabk.append("th%d" % bh)
            out = T.tab[:, 1024 + 64 * bh:1088 + 64 * bh]
            if h == 3:
                lin(out, T.rw[:, 120:184], 1.0, col(32 + rest), rk + ["hb"], [tabk[-1]])
            elif rest:
                ts(out, T.rw[:, 120:184], col(19 + h), col(12 + rest), ALU.add, ALU.add, rk + fk(19 + h, 12 + rest), [tabk[-1]])
            else:
                ts(out, T.rw[:, 120:184], col(8 + h), float(W[h]), ALU.add, ALU.add, rk + fk(8 + h), [tabk[-1]])

    def table_rest():
        table_high(range(8, 16))
        tt(T.hi[:, 16:32], T.lo[:, 16:32], T.rd[:, 0:16], ALU.add, ["lo1", "rd"], ["hi1"])
        tt(T.hi[:, 32:64], T.lo[:, 32:64], T.rd[:, 0:32], ALU.add, ["lo2", "rd"], ["hi2"])
        tabk.append("tl0")
        lin(T.tab[:, 0:64], T.lo[:], 1.0, col(8), ["lo0", "lo1", "lo2"] + fk(8), ["tl0"])
        for j, (o, e) in enumerate(((0, 16), (16, 32), (32, 64))):
            tabk.append("th0%d" % j)
            ts(T.tab[:, 1024 + o:1024 + e], T["hi" if j else "lo"][:, o:e], col(8), float(1 << j), ALU.add, ALU.add,
               ["hi%d" % j if j else "lo0"] + fk(8), [tabk[-1]])

    tt(T.rd[:], T.rw[:, 120:152], T.rw[:, 0:32], ALU.subtract, ["il", "r1", "r2"], ["rd"])
    window_a(0, first[0])
    table_high(range(1, 8))
    quant("uq", "up", 0, 128, T.ub[:], ["ub"], ["uq"])
    upick(first[0])

    def late_rows():
        iota("k16", 0, 64, [[16, 64]], -1024, "k16")
        iota("j16", 0, 64, [[0, 4], [1, 16]], 0, "j16")

    def late_constants():
        fill("half", 0.5)
        fill("eh", 0.0)
        iota("cr", 0, 256, [[0, 2], [1, 128]], 1, "cr")
        diagonal("eh", "half")
        iota("jr", 0, 256, [[1, 256]], 1, "jr")
        ts(col(40), col(7), 0.0, 2.0 ** -20 - 1.0, ALU.is_equal, ALU.mult, fk(7), fk(40))
        ts(col(31), col(5), 0.0, 1024.0 - 2.0 ** -10, ALU.is_equal, ALU.mult, fk(5), fk(31))
        flin(41, 40, 1.0, 1.0)
        flin(42, 24, 256.0, 0.0)
        flin(28, 31, 1.0, 2.0 ** -10)
        flin(26, 24, 2.0, 0.0)
        flin(27, 6, 2.0, -7.0)
        picker("c16", "j16", 5, 1.0, 15.0, 192)
        ts(T.ky[:], T.k16[:], col(5), col(41), ALU.add, ALU.mult, ["k16"] + fk(5, 41), ["ky"])

    def last_constants():
        for b in range(4):
            quant("ehq", "ehp", 128 * b, 128 * b + 128, T.eh[:, 3 - b:515 - b], ["eh"], ["ehq%d" % b])
        quant("vq", "vp", 0, 128, T.vb[:], ["vb"], ["vq"])

    def score(t, k):
        mm(4 + k, "ur", "urp", 128 * k, "xq", "xp", 256 * t, 128, ["ur%d" % k, "us%d" % k, "xqa"])

    def direction(t, k):
        c = 2 * t + k
        scan(T.cm[:, 128 * k:128 * k + 127], ps(4 + k, 1, 128), T.one[:, 0:127], -1e29, ALU.max, ALU.mult, ["one"], ["cm%d" % k], 4 + k)
        op("ac", lambda: A.activation(T.sg[:, 0:127], T.cm[:, 128 * k:128 * k + 127], ACT.Sign, bias=T.cm[:, 128 * k + 126:128 * k + 127],
                                      scale=-1.0, accum_out=T.cnt[:, c:c + 1]), ["cm%d" % k], ["sg", "cnt%d" % c])

    def columns(t, k):
        c = 2 * t + k
        ts(T.to[:, 2 * k:2 * k + 1], T.cnt[:, c:c + 1], 8.0, col(23), ALU.mult, ALU.add, ["cnt%d" % c] + fk(23), ["to%d" % k])

        def rest():
            cp(T.pu[:, 16 * k:16 * k + 16], T.tab[:, 0:2048].indirect(T.to[:, 2 * k:2 * k + 1]), ["to%d" % k] + tabk, ["pu%d" % k])
            acp(T.gr[:, 256 * k:256 * k + 256], T.ew[:, 512 * c:512 * c + 512].indirect(T.pu[:, 16 * k:16 * k + 16]),
                ["ew%d" % c, "pu%d" % k], ["gr%d" % k])
        return rest

    def spread(row, tmp, o, c, step, rkey, out, okey, m, a):
        scan(T[tmp][:, o:o + 256], T[row][:, o:o + 256], T[c][:], 0.0, ALU.max, ALU.mult, [rkey, c], ["s" + okey])
        return lambda: ts(out, T[tmp][:, o + step - 1:o + 256:step], col(m), col(a) if a else -1.0, ALU.mult, ALU.add,
                          ["s" + okey] + fk(m, a), [okey])

    def list64(k):
        return spread("gr", "sc", 256 * k, "c4", 4, "gr%d" % k, T.l64[:, 64 * k:64 * k + 64], "l64%d" % k, 24, 25)

    vk = ["v%d" % b for b in range(4)]

    def decode_x(b):
        tt(T.vt[:, b:1024:4], ps(b, 0, 256), T.tn[:], ALU.mult, ["tn"], [vk[b]], b)

    def low(k, h):
        acp(T.zlow[:, 512 * k + 256 * h:512 * k + 256 * h + 256], T.vt[:, 0:1024].indirect(T.l64[:, 64 * k + 16 * h:64 * k + 16 * h + 16]),
            vk + ["l64%d" % k], ["zw%d%d" % (k, h)])

    def pair_up(t, k):
        for h in range(2):
            o = 512 * k + 256 * h
            tt(T.zt[:, o:o + 256], T.vt[:, 0:1024].indirect(T.l64[:, 64 * k + 32 + 16 * h:64 * k + 48 + 16 * h]), T.zlow[:, o:o + 256],
               ALU.add, vk + ["l64%d" % k, "zw%d%d" % (k, h)], ["zt%d%d" % (k, h)])
        c = 128 * (2 * t + k)
        quant("zq", "zp", c, c + 128, T.zt[:, 512 * k:512 * k + 512], ["zt%d0" % k, "zt%d1" % k], ["zq%d%d" % (t, k)])
        if not (t == TS and k == 0):
            send("z%d%d" % (t, k), "zq%d%d" % (t, k))

    def layer(t, k, bank):
        c = 128 * (2 * t + k)
        home = t == TS and k == 0
        lq, lp, lk = ("wl", "wlp", ["in:wa"]) if home else (("wq", "wp", ["wq", "wp"]), ("mq", "mp", ["mq", "mp"]))[k]
        rq, rp, zk = ("zq", "zp", ["zq%d%d" % (t, k)]) if home else ("zl", "zlp", ["in:z%d%d" % (t, k)])
        for b in range(4):
            mm(bank + b, lq, lp, 128 * b, rq, rp, c, 128, lk + zk)
        for b in range(4):
            ts(T.ht[:, 512 * k + b:512 * k + 512:4], ps(bank + b, 0, 128), 0.03125, None, ALU.mult, w=["ht%d%d" % (k, b)], bank=bank + b)
        quant("hq", "hp", c, c + 128, T.ht[:, 512 * k:512 * k + 512], ["ht%d%d" % (k, b) for b in range(4)], ["hq%d%d" % (t, k)])
        if not home:
            send("h%d%d" % (t, k), "hq%d%d" % (t, k))

    def both_signs(x, h):
        for s in range(2):
            o = 1024 * s + 512 * h
            acp(T.xx[:, o:o + 512], T[x][:, 512 * h:512 * h + 512], ["x" + "ab"[h]], ["xx%d%d" % (s, h)], scale=0.5 - s)

    def turn_list():
        scan(T.sf[:], T.fl[:], T.c4[:], 0.0, ALU.max, ALU.mult, ["fl", "c4"], ["sf"])
        tt(T.ty[:], T.sf[:, 3:256:4], T.ky[:], ALU.add, ["sf", "ky"], ["ty"])
        ts(T.ly[:], T.ty[:], col(42), None, ALU.mult, r=["ty"] + fk(42), w=["ly"])

    def turned(h):
        acp(T.yh[:, 512 * h:512 * h + 512], T.xx[:, 0:2048].indirect(T.ly[:, 32 * h:32 * h + 32]),
            ["xx00", "xx01", "xx10", "xx11", "ly"], ["y%d" % h])

    def y_in_pairs(s):
        acp(T.yp[:, 512 * s:512 * s + 512], T.yh[:, 0:1024].indirect(T.l64[:, 32 * s:32 * s + 32]), ["y0", "y1", "l640"], ["yp%d" % s])

    def pair_numbers():
        for f in [spread("gr", "s16", 256 * k, "c16", 16, "gr%d" % k, T.l16[:, 16 * k:16 * k + 16], "l16%d" % k, 28, 0) for k in (1, 0)]:
            f()
        cp(T.nr[:, 0:256].indirect(T.l16[:, 16:32]), T.cr[:], ["cr", "l161"], ["nr"])
        acp(T.nc[:], T.nr[:, 0:256].indirect(T.l16[:, 0:16]), ["nr", "l160"], ["nc"])

    def positions():
        cp(T.pos[:, 0:256].indirect(T.l16[:, 0:16]), T.jr[:], ["jr", "l160"], ["pos"])
        for f in [spread("nc", "sn", 0, "c4", 4, "nc", T.n1[:], "n1", 24, 25), spread("pos", "sp", 0, "c4", 4, "pos", T.pl0[:], "pl0", 26, 27)]:
            f()

    def decode_h(t, k, bank):
        c = 128 * (2 * t + k)
        home = t == TS and k == 0
        rq, rp, hk = ("hq", "hp", ["hq%d%d" % (t, k)]) if home else ("hl", "hlp", ["in:h%d%d" % (t, k)])
        for b in range(4):
            mm(bank + b, "ehq", "ehp", 128 * b, rq, rp, c, 128, ["ehq%d" % b] + hk)

    def bounds(bank):
        for s in range(2):
            for b in range(4):
                o = 1024 * s + 2 * b + 1
                y = T.yp[:, 512 * s + b:512 * s + 512:4]
                tt(T.u0[:, o:1024 * s + 1024:8], ps(bank + b, 0, 128), y, ALU.min, ["yp%d" % s], ["ua%d%d" % (s, b)], bank + b)
                tt(T.u1[:, o:1024 * s + 1024:8], ps(bank + b, 0, 128), y, ALU.max, ["yp%d" % s], ["ub%d%d" % (s, b)], bank + b)

    dk = ["d1%d" % b for b in range(4)]

    def pick_d1(c, f):
        f(T.u0[:, 512 * c:512 * c + 512:2], T.d1[:, 0:512].indirect(T.n1[:, 16 * c:16 * c + 16]), dk + ["n1"], ["ea%d" % c])

    def middle(c):
        cp(T.u1[:, 512 * c:512 * c + 512:2], T.u0[:, 512 * c:512 * c + 512:2], ["ea%d" % c], ["eb%d" % c])
        return lambda: scan(T.mm[:, 512 * c:512 * c + 512], T.u0[:, 512 * c:512 * c + 512], T.u1[:, 512 * c:512 * c + 512], 0.0, ALU.max, ALU.min,
                            ["ea%d" % c, "eb%d" % c] + ["u%s%d%d" % (a, c // 2, b) for a in "ab" for b in range(4)], ["mm%d" % c])

    def new_state(h):
        tt(T.xt[:, 512 * h:512 * h + 512], T.mm[:, 0:2048].indirect(T.pl0[:, 32 * h:32 * h + 32]), T.yh[:, 512 * h:512 * h + 512], ALU.add,
           ["mm%d" % c for c in range(4)] + ["pl0", "y%d" % h], ["x" + "ab"[h]])

    def quant_x(t, h):
        quant("xq", "xp", 256 * t + 128 * h, 256 * t + 128 * h + 128, T["xt" if t else "x0"][:, 512 * h:512 * h + 512],
              ["x" + "ab"[h]], ["xq" + "ab"[h]])

    for t in range(R):
        x = "xt" if t else "x0"
        a, b = first[t], 1 - first[t]
        home = t == TS
        quant_x(t, 0)
        score(t, a)
        if t:
            score(t, b)
            both_signs(x, 0)
            new_state(1)
        else:
            upick(2)
        quant_x(t, 1)
        mm(6, "ur", "urp", 256, "xq", "xp", 256 * t, 256, ["ur2", "us2", "xqa", "xqb"])
        if not t:
            upick(b)
            score(t, b)
        for j in range(4):
            mm(j, "e1q", "e1p", 128 * j, "xq", "xp", 256 * t, 256, ["e1q%d" % j, "xqa", "xqb"])
        if not t:
            table_rest()
        direction(t, a)
        if not t:
            window_b(0, a)
            window_a(0, b)
        direction(t, b)
        f = columns(t, a)
        ts(T.tn[:], ps(6, 0, 256), 0.0, 0.5, ALU.is_gt, ALU.subtract, w=["tn"], bank=6)
        f()
        if not t:
            window_b(0, b)
        f = columns(t, b)
        decode_x(0)
        f()
        lin(T.fl[:], T.tn[:], -1.0, 1.5, ["tn"], ["fl"])
        decode_x(1)
        f = list64(a)
        decode_x(2)
        f()
        f = list64(b)
        decode_x(3)
        low(a, 0)
        low(a, 1)
        f()
        low(b, 0)
        low(b, 1)
        if t:
            turn_list()
            both_signs(x, 1)
        pair_up(t, a)
        if not t:
            late_rows()
            both_signs(x, 0)
            both_signs(x, 1)
        pair_up(t, b)
        if not t:
            late_constants()
        if t == R - 1:
            lin(T.odb[:], T.cnt[:], 1.0, 1.0, ["cnt%d" % c for c in range(2 * R)], ["odb"])
            for j in range(8):
                dma("sy", T.od[j:j + 1, :], T.odb[16 * j:16 * j + 1, :], r=["odb"])
        if home:
            layer(t, 0, 4)
            decode_h(t, 0, 4)
        if not t:
            turn_list()
            last_constants()
        turned(0)
        turned(1)
        y_in_pairs(0)
        y_in_pairs(1)
        for step in plan[rank][t]:
            if step == "lend":
                if not home:
                    layer(t, 0, 4)
                layer(t, 1, 0)
            elif step == "pairs":
                pair_numbers()
                if not t:
                    window_a(1, 0)
                    window_a(1, 1)
            elif step == "positions":
                positions()
            elif step == "windows":
                window_b(t + 1, 0)
                window_b(t + 1, 1)
            else:
                if not home:
                    decode_h(t, 0, 4)
                bounds(4)
        decode_h(t, 1, 0)
        for j in range(4):
            (cp if home and j % 2 else acp)(T.d1[:, j:512:4], ps(j, 0, 128), w=[dk[j]], bank=j)
        order = (3, 0, 1, 2) if home else (0, 1, 2, 3)
        for c in order:
            pick_d1(c, cp if home and c == 3 else acp)
        if t + 2 < R:
            window_a(t + 2, 0)
            window_a(t + 2, 1)
        m = middle(order[0])
        for c in order[1:]:
            nxt = middle(c)
            m()
            m = nxt
        m()
        new_state(0)

    for h in range(2):
        if h:
            new_state(1)
        quant_x(R, h)
        c = 256 * R + 128 * h
        mm(6 + h, "vq", "vp", 0, "xq", "xp", c, 128, ["vq", "xq" + "ab"[h]])
        dma("sy", T.oc[:, 512 * h:512 * h + 512], T.xq[:, c:c + 128].bitcast(dt.uint8), r=["xq" + "ab"[h]])
        acp(T.yo[:, 128 * h:128 * h + 128], ps(6 + h, 0, 128), w=["yo%d" % h], bank=6 + h)
        dma("ac", T.y[:, 128 * h:128 * h + 128], T.yo[:, 128 * h:128 * h + 128], r=["yo%d" % h])
    for j in range(4):
        dma("sy", T.osc[4 * j:4 * j + 4, :], T.xp[32 * j:32 * j + 4, 256 * R:256 * R + 256], r=["xqa", "xqb"])
    for sem in total:
        if waited.get(sem, 0) < total[sem]:
            g.wait_ge(T.sem[sem], total[sem])
